import numpy as np
import ml_dtypes


def mxq(x, axis, fmt="e4m3"):
    dtype, down = {"e4m3": (ml_dtypes.float8_e4m3fn, 7), "e5m2": (ml_dtypes.float8_e5m2, 14)}[fmt]
    v = np.moveaxis(np.asarray(x, np.float32).astype(ml_dtypes.bfloat16).astype(np.float64), axis, -1)
    blocks = v.reshape(v.shape[:-1] + (-1, 32))
    amax = np.abs(blocks).max(-1, keepdims=True)
    byte = np.maximum(np.where(amax > 0, np.frexp(amax)[1] - 1 + 127, 0) - down, 1)
    scale = np.exp2(byte - 127.0)
    codes = (blocks / scale).astype(np.float32).astype(dtype).astype(np.float64)
    return np.moveaxis((codes * scale).reshape(v.shape), -1, axis)


WIDE = False


def mx_kscale(k):
    if not WIDE:
        return np.ones(k)
    levels = np.array([10, -10, 5, -5, 0])
    if k % 512:
        return np.exp2(np.random.permutation(np.resize(levels, k // 32))).repeat(32)
    a = np.empty((k // 512, 16))
    for p in range(k // 512):
        a[p, :8] = np.random.permutation(np.resize(levels, 8))
        for g in range(8):
            far = levels[np.abs(levels - a[p, g]) >= 10]
            a[p, g + 8] = far[np.random.randint(len(far))]
    return np.exp2(a.ravel()).repeat(32)


def f64(x):
    return np.asarray(x).astype(np.float64)


def striped(idx):
    return np.tile(np.asarray(idx).reshape(-1, 16).T, (8, 1)).astype(np.uint16)


def unstriped(offs):
    return offs[:16].T.reshape(-1).astype(np.int64)


E2M1 = np.array([0.0, 0.5, 1.0, 1.5, 2.0, 3.0, 4.0, 6.0, -0.0, -0.5, -1.0, -1.5, -2.0, -3.0, -4.0, -6.0])


def pack_weight(w, fmt):
    k, n = w.shape
    w = f64(np.asarray(w, np.float32).astype(ml_dtypes.bfloat16)).reshape(k // 32, 32, n)
    amax = np.abs(w).max(1)
    if fmt == "e4m3":
        byte = np.frexp(amax)[1] - 1 + 127 - 7
    else:
        mant, ex = np.frexp(amax / 6.0)
        byte = np.where(mant > 0.5, ex, ex - 1) + 127
    byte = np.clip(np.where(amax > 0, byte, 1), 1, 254)
    scaled = (w * np.exp2(127.0 - byte)[:, None, :]).reshape(k, n).astype(np.float32)
    by_word = np.ascontiguousarray(scaled.reshape(k // 512, 128, 4, n).transpose(0, 1, 3, 2))
    if fmt == "e4m3":
        words = by_word.astype(ml_dtypes.float8_e4m3fn).view(np.uint8)
    else:
        c = by_word.astype(ml_dtypes.float4_e2m1fn).view(np.uint8) & 0xF
        words = (c[..., 0::2] | (c[..., 1::2] << 4)).reshape(k // 512, 128, 2 * n)
    return np.ascontiguousarray(words), np.ascontiguousarray(byte.astype(np.uint8).reshape(k // 512, 16, n))


def unpack_weight(words, scales, fmt):
    g, _, n = scales.shape
    words = np.ascontiguousarray(words).reshape(g, 128, n, -1)
    if fmt == "e4m3":
        vals = words.view(ml_dtypes.float8_e4m3fn).astype(np.float64)
    else:
        nib = np.empty((g, 128, n, 4), np.uint8)
        nib[..., 0::2] = words & 0xF
        nib[..., 1::2] = words >> 4
        vals = E2M1[nib]
    vals = vals * np.repeat(np.exp2(scales.astype(np.float64) - 127.0), 8, axis=1)[..., None]
    return vals.transpose(0, 1, 3, 2).reshape(g * 512, n)


def bf(x):
    return np.asarray(x, np.float32).astype(ml_dtypes.bfloat16)


def planes(Y):
    r, m = Y.shape
    b = f64(bf(Y)).reshape(r // 32, 32, m)
    amax = np.abs(b).max(1)
    byte = np.clip(np.where(amax > 0, np.frexp(amax)[1] - 1 + 127 - 7, 1), 1, 254)
    codes = (b * np.exp2(127.0 - byte)[:, None, :]).reshape(r, m).astype(np.float32).astype(ml_dtypes.float8_e4m3fn).view(np.uint8)
    words = codes.reshape(r // 512, 128, 4, m).transpose(0, 1, 3, 2)
    return np.ascontiguousarray(words), np.ascontiguousarray(byte.astype(np.uint8).reshape(r // 512, 16, m))


D, T, I, Q, E, M, C = 512, 2048, 512, 256, 512, 1024, 512


def setup_inputs():
    n = np.random.standard_normal
    idx = np.random.permutation(T)[:I]
    idx2 = np.random.permutation(T)[:I]
    idx3 = np.random.permutation(T)[:I]
    idx4 = np.random.permutation(M)[:Q]
    fd = mx_kscale(D)
    fi = mx_kscale(I)
    fc = mx_kscale(C)
    ti = np.ones(T)
    ti[idx] = fi
    keysp = pack_weight(n((D, T)) / fd[:, None], "e2m1")
    return {
        "query": (n((D, Q)) * 1.2 / np.sqrt(D) * fd[:, None]).astype(np.float32),
        "keys_words": keysp[0],
        "keys_scales": keysp[1],
        "lam": (np.random.uniform(0.2, 0.7, (Q, 1))).astype(np.float32),
        "os": (np.random.uniform(0.02, 0.08, (1, I)) * fi).astype(np.float32),
        "vals": (n((E, T)) / ti).astype(np.float32),
        "wm": (n((C, E)) * 1.0 / np.sqrt(C) * fc[:, None]).astype(np.float32),
        "mstore": (n((C, M)) / fc[:, None]).astype(np.float32),
        "offs": striped(idx),
        "offs2": striped(idx2),
        "offs3": striped(idx3),
        "offs4": striped(idx4),
    }


def reference(query, keys_words, keys_scales, lam, os, vals, wm, mstore, offs, offs2, offs3, offs4):
    idx = unstriped(offs)
    idx2 = unstriped(offs2)
    idx3 = unstriped(offs3)
    idx4 = unstriped(offs4)
    keysu = unpack_weight(keys_words, keys_scales, "e2m1")
    queryq = mxq(f64(query), 0, "e4m3")
    a = queryq.T @ keysu
    mx3 = np.maximum(np.maximum(a[:, idx], a[:, idx2]), a[:, idx3])
    mn3 = np.minimum(np.minimum(a[:, idx], a[:, idx2]), a[:, idx3])
    s = (a[:, idx] + a[:, idx2] + a[:, idx3]) / 3.0 - (mx3 - mn3) * f64(lam)
    w = np.maximum(s, 0.0)
    wo1 = w * f64(os)
    wt1 = wo1.T
    vt1 = f64(vals)[:, idx].T
    vt1q = mxq(vt1, 0, "e4m3")
    wt1q = mxq(wt1, 0, "e4m3")
    o = vt1q.T @ wt1q
    wmq = mxq(f64(wm), 0, "e4m3")
    mstoreq = mxq(f64(mstore), 0, "e4m3")
    me = wmq.T @ mstoreq
    y = o * me[:, idx4]
    words, scales = planes(y)
    return y, words, scales

@@ -1,0 +1,232 @@
+from contextlib import ExitStack
+
+import concourse.mybir as mybir
+from concourse.masks import make_identity
+
+D, T, I, Q, E, M, C = 512, 2048, 512, 256, 512, 1024, 512
+FLOPS = 2 * (D * Q * T + I * E * Q + C * E * M)
+
+F32 = mybir.dt.float32
+BF16 = mybir.dt.bfloat16
+I32 = mybir.dt.int32
+U32 = mybir.dt.uint32
+U16 = mybir.dt.uint16
+U8 = mybir.dt.uint8
+FP8X4 = mybir.dt.float8_e4m3fn_x4
+FP4X4 = mybir.dt.float4_e2m1fn_x4
+ALU = mybir.AluOpType
+COPY = mybir.ActivationFunctionType.Copy
+
+P = 128
+PACK = 4
+BANK = 512
+QT = Q // P
+
+
+def interleave(nc, grouped, raw):
+    nc.vector.tensor_copy(
+        out=grouped.rearrange("p (c i) t -> p c t i", i=4),
+        in_=raw.rearrange("p t (c i) -> p c t i", i=4),
+    )
+
+
+def quantize(nc, codes, scales, grouped):
+    nc.vector.quantize_mx(out=codes.bitcast(FP8X4), scales=scales, in_=grouped.rearrange("p c t -> p (c t)"))
+
+
+def tile_attend_spreadof3_remembered_lean_pl_kernel(
+    tc, query, keys_words, keys_scales, lam, slot_factor, vals, wm, mstore, offs, offs2, offs3, offs4, out_0, out_1, out_2
+):
+    nc = tc.nc
+    with ExitStack() as ctx:
+        sb = ctx.enter_context(tc.tile_pool(name="sb", bufs=1))
+        ps_mm = ctx.enter_context(tc.psum_pool(name="ps_mm", bufs=4))
+        ps_tr = ctx.enter_context(tc.psum_pool(name="ps_tr", bufs=2))
+        ps_o = ctx.enter_context(tc.psum_pool(name="ps_o", bufs=2))
+
+        def tile(shape, dtype, name):
+            return sb.tile(shape, dtype, name=name, align_bytes=64)
+
+        lists = [tile([P, I // 16], U16, "list%d" % j) for j in range(3)]
+        list_mem = tile([P, Q // 16], U16, "list_mem")
+        q_raw = tile([P, PACK, Q], F32, "q_raw")
+        k_words = tile([P, 2 * T], U8, "k_words")
+        k_scales = tile([P, T], U8, "k_scales")
+        wm_raw = tile([P, PACK, E], F32, "wm_raw")
+        ms_raw = [tile([P, PACK, BANK], F32, "ms_raw%d" % n) for n in range(M // BANK)]
+        v_raw = [tile([P, T], F32, "v_raw%d" % t) for t in range(PACK)]
+        lam_raw = tile([P, QT], F32, "lam_raw")
+        os_raw = tile([P, PACK], F32, "os_raw")
+        ident = tile([P, P], F32, "ident")
+
+        nc.vector.memset(k_scales[:].bitcast(I32), 0)
+        nc.sync.dma_start(out=q_raw[:], in_=query.rearrange("(p t) q -> p t q", t=PACK))
+        nc.sync.dma_start(out=k_words[:].bitcast(I32), in_=keys_words[0].bitcast(I32))
+        for g in range(4):
+            nc.sync.dma_start(
+                out=k_scales[32 * g : 32 * g + 4, :].bitcast(I32), in_=keys_scales[0, 4 * g : 4 * g + 4, :].bitcast(I32)
+            )
+        with nc.allow_non_contiguous_dma(reason="one factor a partition"):
+            nc.gpsimd.dma_start(out=lam_raw[:], in_=lam.rearrange("(h p) o -> p (h o)", p=P))
+        nc.gpsimd.dma_start(out=os_raw[:], in_=slot_factor.rearrange("o (p t) -> p (o t)", t=PACK))
+        make_identity(nc, ident[:])
+        ms_rows = mstore.rearrange("(p t) m -> p t m", t=PACK)
+        v_rows = vals.rearrange("(p t) x -> p t x", t=PACK)
+        nc.sync.dma_start(out=wm_raw[:], in_=wm.rearrange("(p t) e -> p t e", t=PACK))
+        nc.sync.dma_start(out=ms_raw[0][:], in_=ms_rows[:, :, 0:BANK])
+        for dst, src in zip(lists, (offs, offs2, offs3)):
+            nc.sync.dma_start(dst[:], src)
+        nc.sync.dma_start(out=ms_raw[1][:], in_=ms_rows[:, :, BANK : 2 * BANK])
+        nc.sync.dma_start(list_mem[:], offs4)
+        for t in range(PACK):
+            nc.sync.dma_start(out=v_raw[t][:], in_=v_rows[:, t, :])
+
+        lam_neg = tile([P, QT], F32, "lam_neg")
+        lam_pos = tile([P, QT], F32, "lam_pos")
+        os_third = tile([P, PACK], F32, "os_third")
+        nc.gpsimd.tensor_scalar(lam_neg[:], lam_raw[:], -3.0, 0.0, ALU.mult, ALU.add)
+        nc.gpsimd.tensor_scalar(lam_pos[:], lam_raw[:], 3.0, 0.0, ALU.mult, ALU.add)
+        nc.gpsimd.tensor_scalar(os_third[:], os_raw[:], 1.0 / 3.0, 0.0, ALU.mult, ALU.add)
+
+        q_bf = [tile([P, P, PACK], BF16, "q_bf%d" % h) for h in range(QT)]
+        q_codes = [tile([P, P], U32, "q_codes%d" % h) for h in range(QT)]
+        q_scales = [tile([P, P], U8, "q_scales%d" % h) for h in range(QT)]
+        for h in range(QT):
+            interleave(nc, q_bf[h][:], q_raw[:, :, h * P : (h + 1) * P])
+        for h in range(QT):
+            quantize(nc, q_codes[h][:], q_scales[h][:], q_bf[h][:])
+
+        a_sb = [tile([P, T], F32, "a_sb%d" % h) for h in range(QT)]
+        picked = [[tile([P, I], F32, "picked%d_%d" % (h, j)) for j in range(3)] for h in range(QT)]
+        for h in range(QT):
+            for n in range(T // BANK):
+                bank = ps_mm.tile([P, BANK], F32, name="mm")
+                nc.tensor.matmul_mx(
+                    out=bank[:],
+                    lhsT=q_codes[h][:].bitcast(FP8X4),
+                    lhsT_scale=q_scales[h][:],
+                    rhs=k_words[:, 2 * BANK * n : 2 * BANK * (n + 1)].bitcast(FP4X4),
+                    rhs_scale=k_scales[:, BANK * n : BANK * (n + 1)],
+                    start=True,
+                    stop=True,
+                )
+                dst = a_sb[h][:, BANK * n : BANK * (n + 1)]
+                if n % 2 == 0:
+                    nc.scalar.activation(dst, bank[:], COPY)
+                else:
+                    nc.vector.tensor_copy(dst, bank[:])
+            for j in range(3):
+                nc.scalar.activation(picked[h][j][:], a_sb[h][:].indirect(lists[j][:]), COPY)
+
+        wm_bf = tile([P, E, PACK], BF16, "wm_bf")
+        wm_codes = tile([P, E], U32, "wm_codes")
+        wm_scales = tile([P, E], U8, "wm_scales")
+        nc.vector.tensor_copy(
+            out=wm_bf[:].rearrange("p (t m) j -> p m j t", t=PACK),
+            in_=wm_raw[:].rearrange("p j (m t) -> p m j t", t=PACK),
+        )
+        ms_bf = [tile([P, BANK, PACK], BF16, "ms_bf%d" % n) for n in range(M // BANK)]
+        ms_codes = [tile([P, BANK], U32, "ms_codes%d" % n) for n in range(M // BANK)]
+        ms_scales = [tile([P, BANK], U8, "ms_scales%d" % n) for n in range(M // BANK)]
+        me_sb = [tile([P, M], F32, "me_sb%d" % t) for t in range(PACK)]
+        me_picked = [tile([P, Q], F32, "me_picked%d" % t) for t in range(PACK)]
+
+        def memories(n):
+            for t in range(PACK):
+                bank = ps_mm.tile([P, BANK], F32, name="mm")
+                nc.tensor.matmul_mx(
+                    out=bank[:],
+                    lhsT=wm_codes[:, P * t : P * (t + 1)].bitcast(FP8X4),
+                    lhsT_scale=wm_scales[:, P * t : P * (t + 1)],
+                    rhs=ms_codes[n][:].bitcast(FP8X4),
+                    rhs_scale=ms_scales[n][:],
+                    start=True,
+                    stop=True,
+                )
+                nc.scalar.activation(me_sb[t][:, BANK * n : BANK * (n + 1)], bank[:], COPY)
+
+        w_bf = [tile([P, P, PACK], BF16, "w_bf%d" % h) for h in range(QT)]
+        w_codes = tile([P, Q], U32, "w_codes")
+        w_scales = tile([P, Q], U8, "w_scales")
+
+        def weights(h):
+            g1, g2, g3 = picked[h]
+            hi2 = tile([P, I], F32, "hi2_%d" % h)
+            lo2 = tile([P, I], F32, "lo2_%d" % h)
+            hi3 = tile([P, I], F32, "hi3_%d" % h)
+            lo3 = tile([P, I], F32, "lo3_%d" % h)
+            up = tile([P, I], F32, "up_%d" % h)
+            down = tile([P, I], F32, "down_%d" % h)
+            nc.vector.tensor_tensor(hi2[:], g1[:], g2[:], ALU.max)
+            nc.vector.tensor_tensor(lo2[:], g1[:], g2[:], ALU.min)
+            nc.vector.tensor_tensor(hi3[:], hi2[:], g3[:], ALU.max)
+            nc.vector.tensor_tensor(lo3[:], lo2[:], g3[:], ALU.min)
+            nc.vector.scalar_tensor_tensor(up[:], hi3[:], lam_neg[:, h : h + 1], hi2[:], ALU.mult, ALU.add)
+            nc.vector.scalar_tensor_tensor(down[:], lo3[:], lam_pos[:, h : h + 1], lo2[:], ALU.mult, ALU.add)
+            bank = ps_tr.tile([P, PACK, P], F32, name="tr")
+            for r in range(PACK):
+                for j, term in enumerate((g3, up, down)):
+                    nc.tensor.matmul(
+                        bank[:, r, :], term[:, r:I:PACK], ident[:], start=(j == 0), stop=(j == 2), is_transpose=True
+                    )
+            nc.vector.scalar_tensor_tensor(
+                w_bf[h][:],
+                bank[:].rearrange("p r q -> p q r"),
+                0.0,
+                os_third[:].unsqueeze(1).to_broadcast([P, P, PACK]),
+                ALU.max,
+                ALU.mult,
+            )
+            quantize(nc, w_codes[:, P * h : P * (h + 1)], w_scales[:, P * h : P * (h + 1)], w_bf[h][:])
+
+        interleave(nc, ms_bf[0][:], ms_raw[0][:])
+        quantize(nc, wm_codes[:], wm_scales[:], wm_bf[:])
+        quantize(nc, ms_codes[0][:], ms_scales[0][:], ms_bf[0][:])
+        memories(0)
+        weights(0)
+        interleave(nc, ms_bf[1][:], ms_raw[1][:])
+        quantize(nc, ms_codes[1][:], ms_scales[1][:], ms_bf[1][:])
+        memories(1)
+        weights(1)
+
+        y = tile([P, PACK, Q], F32, "y")
+        y_rows = out_0.rearrange("(p t) q -> p t q", t=PACK)
+        for t in range(PACK):
+            v_picked = tile([P, I], BF16, "v_picked%d" % t)
+            nc.scalar.activation(me_picked[t][:], me_sb[t][:].indirect(list_mem[:]), COPY)
+            nc.scalar.activation(v_picked[:], v_raw[t][:].indirect(lists[0][:]), COPY)
+            pairs = v_picked[:].bitcast(F32)
+            turned = ps_tr.tile([P, 2, P], F32, name="tr")
+            for u in range(2):
+                nc.tensor.transpose(turned[:, u, :], pairs[:, u : I // 2 : 2], ident[:])
+            vt_bf = tile([P, P, PACK], BF16, "vt_bf%d" % t)
+            vt_codes = tile([P, P], U32, "vt_codes%d" % t)
+            vt_scales = tile([P, P], U8, "vt_scales%d" % t)
+            nc.vector.tensor_copy(out=vt_bf[:].bitcast(F32), in_=turned[:].rearrange("p u e -> p e u"))
+            quantize(nc, vt_codes[:], vt_scales[:], vt_bf[:])
+            o = ps_o.tile([P, Q], F32, name="o")
+            nc.tensor.matmul_mx(
+                out=o[:],
+                lhsT=vt_codes[:].bitcast(FP8X4),
+                lhsT_scale=vt_scales[:],
+                rhs=w_codes[:].bitcast(FP8X4),
+                rhs_scale=w_scales[:],
+                start=True,
+                stop=True,
+            )
+            nc.vector.tensor_tensor(y[:, t, :], o[:], me_picked[t][:], ALU.mult)
+            nc.sync.dma_start(out=y_rows[:, t, :], in_=y[:, t, :])
+
+        y_bf = tile([P, Q, PACK], BF16, "y_bf")
+        y_codes = tile([P, Q], U32, "y_codes")
+        y_scales = tile([P, Q], U8, "y_scales")
+        interleave(nc, y_bf[:], y[:])
+        quantize(nc, y_codes[:], y_scales[:], y_bf[:])
+        nc.scalar.dma_start(
+            out=out_1[0].rearrange("p c r -> p (c r)").bitcast(I32), in_=y_codes[:].bitcast(I32)
+        )
+        for g in range(4):
+            queue = nc.sync if g % 2 == 0 else nc.scalar
+            queue.dma_start(
+                out=out_2[0, 4 * g : 4 * g + 4, :].bitcast(I32), in_=y_scales[32 * g : 32 * g + 4, :].bitcast(I32)
+            )

@@ -40,9 +40,7 @@ def tile_attend_spreadof3_remembered_lean_pl_kernel(
     nc = tc.nc
     with ExitStack() as ctx:
         sb = ctx.enter_context(tc.tile_pool(name="sb", bufs=1))
-        ps_mm = ctx.enter_context(tc.psum_pool(name="ps_mm", bufs=4))
-        ps_tr = ctx.enter_context(tc.psum_pool(name="ps_tr", bufs=2))
-        ps_o = ctx.enter_context(tc.psum_pool(name="ps_o", bufs=2))
+        ps = ctx.enter_context(tc.psum_pool(name="ps", bufs=1))
 
         def tile(shape, dtype, name):
             return sb.tile(shape, dtype, name=name, align_bytes=64)
@@ -73,13 +71,15 @@ def tile_attend_spreadof3_remembered_lean_pl_kernel(
         ms_rows = mstore.rearrange("(p t) m -> p t m", t=PACK)
         v_rows = vals.rearrange("(p t) x -> p t x", t=PACK)
         nc.sync.dma_start(out=wm_raw[:], in_=wm.rearrange("(p t) e -> p t e", t=PACK))
-        nc.sync.dma_start(out=ms_raw[0][:], in_=ms_rows[:, :, 0:BANK])
         for dst, src in zip(lists, (offs, offs2, offs3)):
             nc.sync.dma_start(dst[:], src)
-        nc.sync.dma_start(out=ms_raw[1][:], in_=ms_rows[:, :, BANK : 2 * BANK])
+        nc.sync.dma_start(out=ms_raw[0][:], in_=ms_rows[:, :, 0 * BANK : (0 + 1) * BANK])
+        nc.sync.dma_start(out=v_raw[0][:], in_=v_rows[:, 0, :])
+        nc.sync.dma_start(out=ms_raw[1][:], in_=ms_rows[:, :, 1 * BANK : (1 + 1) * BANK])
         nc.sync.dma_start(list_mem[:], offs4)
-        for t in range(PACK):
-            nc.sync.dma_start(out=v_raw[t][:], in_=v_rows[:, t, :])
+        nc.sync.dma_start(out=v_raw[1][:], in_=v_rows[:, 1, :])
+        nc.sync.dma_start(out=v_raw[2][:], in_=v_rows[:, 2, :])
+        nc.sync.dma_start(out=v_raw[3][:], in_=v_rows[:, 3, :])
 
         lam_neg = tile([P, QT], F32, "lam_neg")
         lam_pos = tile([P, QT], F32, "lam_pos")
@@ -100,7 +100,7 @@ def tile_attend_spreadof3_remembered_lean_pl_kernel(
         picked = [[tile([P, I], F32, "picked%d_%d" % (h, j)) for j in range(3)] for h in range(QT)]
         for h in range(QT):
             for n in range(T // BANK):
-                bank = ps_mm.tile([P, BANK], F32, name="mm")
+                bank = ps.tile([P, BANK], F32, name="bank%d" % (4 * h + n))
                 nc.tensor.matmul_mx(
                     out=bank[:],
                     lhsT=q_codes[h][:].bitcast(FP8X4),
@@ -111,7 +111,7 @@ def tile_attend_spreadof3_remembered_lean_pl_kernel(
                     stop=True,
                 )
                 dst = a_sb[h][:, BANK * n : BANK * (n + 1)]
-                if n % 2 == 0:
+                if h == 0 and n % 2 == 0:
                     nc.scalar.activation(dst, bank[:], COPY)
                 else:
                     nc.vector.tensor_copy(dst, bank[:])
@@ -129,11 +129,11 @@ def tile_attend_spreadof3_remembered_lean_pl_kernel(
         ms_codes = [tile([P, BANK], U32, "ms_codes%d" % n) for n in range(M // BANK)]
         ms_scales = [tile([P, BANK], U8, "ms_scales%d" % n) for n in range(M // BANK)]
         me_sb = [tile([P, M], F32, "me_sb%d" % t) for t in range(PACK)]
-        me_picked = [tile([P, Q], F32, "me_picked%d" % t) for t in range(PACK)]
+        me_picked = tile([P, PACK, Q], F32, "me_picked")
 
         def memories(n):
             for t in range(PACK):
-                bank = ps_mm.tile([P, BANK], F32, name="mm")
+                bank = ps.tile([P, BANK], F32, name="bank%d" % (4 * n + t))
                 nc.tensor.matmul_mx(
                     out=bank[:],
                     lhsT=wm_codes[:, P * t : P * (t + 1)].bitcast(FP8X4),
@@ -143,7 +143,11 @@ def tile_attend_spreadof3_remembered_lean_pl_kernel(
                     start=True,
                     stop=True,
                 )
-                nc.scalar.activation(me_sb[t][:, BANK * n : BANK * (n + 1)], bank[:], COPY)
+                dst = me_sb[t][:, BANK * n : BANK * (n + 1)]
+                if True:
+                    nc.scalar.activation(dst, bank[:], COPY)
+                else:
+                    nc.vector.tensor_copy(dst, bank[:])
 
         w_bf = [tile([P, P, PACK], BF16, "w_bf%d" % h) for h in range(QT)]
         w_codes = tile([P, Q], U32, "w_codes")
@@ -155,20 +159,28 @@ def tile_attend_spreadof3_remembered_lean_pl_kernel(
             lo2 = tile([P, I], F32, "lo2_%d" % h)
             hi3 = tile([P, I], F32, "hi3_%d" % h)
             lo3 = tile([P, I], F32, "lo3_%d" % h)
-            up = tile([P, I], F32, "up_%d" % h)
-            down = tile([P, I], F32, "down_%d" % h)
+            up = tile([P, PACK, P], F32, "up_%d" % h)
+            down = tile([P, PACK, P], F32, "down_%d" % h)
             nc.vector.tensor_tensor(hi2[:], g1[:], g2[:], ALU.max)
             nc.vector.tensor_tensor(lo2[:], g1[:], g2[:], ALU.min)
             nc.vector.tensor_tensor(hi3[:], hi2[:], g3[:], ALU.max)
             nc.vector.tensor_tensor(lo3[:], lo2[:], g3[:], ALU.min)
-            nc.vector.scalar_tensor_tensor(up[:], hi3[:], lam_neg[:, h : h + 1], hi2[:], ALU.mult, ALU.add)
-            nc.vector.scalar_tensor_tensor(down[:], lo3[:], lam_pos[:, h : h + 1], lo2[:], ALU.mult, ALU.add)
-            bank = ps_tr.tile([P, PACK, P], F32, name="tr")
-            for r in range(PACK):
-                for j, term in enumerate((g3, up, down)):
-                    nc.tensor.matmul(
-                        bank[:, r, :], term[:, r:I:PACK], ident[:], start=(j == 0), stop=(j == 2), is_transpose=True
-                    )
+            for term, end3, factor, end2 in ((up, hi3, lam_neg, hi2), (down, lo3, lam_pos, lo2)):
+                nc.vector.scalar_tensor_tensor(
+                    term[:].rearrange("p r s -> p s r"),
+                    end3[:].rearrange("p (s r) -> p s r", r=PACK),
+                    factor[:, h : h + 1],
+                    end2[:].rearrange("p (s r) -> p s r", r=PACK),
+                    ALU.mult,
+                    ALU.add,
+                )
+            bank = ps.tile([P, PACK, P], F32, name="bank%d" % (h))
+            terms = [(r, up[:, r, :]) for r in range(PACK)] + [(r, g3[:, r:I:PACK]) for r in range(PACK)]
+            terms = terms + [(r, down[:, r, :]) for r in range(PACK)]
+            for j, (r, term) in enumerate(terms):
+                nc.tensor.matmul(
+                    bank[:, r, :], term, ident[:], start=(j == 0), stop=(j == len(terms) - 1), is_transpose=True
+                )
             nc.vector.scalar_tensor_tensor(
                 w_bf[h][:],
                 bank[:].rearrange("p r q -> p q r"),
@@ -179,6 +191,46 @@ def tile_attend_spreadof3_remembered_lean_pl_kernel(
             )
             quantize(nc, w_codes[:, P * h : P * (h + 1)], w_scales[:, P * h : P * (h + 1)], w_bf[h][:])
 
+        vt_codes = tile([P, E], U32, "vt_codes")
+        vt_scales = tile([P, E], U8, "vt_scales")
+
+        def values(t):
+            v_picked = tile([P, I], BF16, "v_picked%d" % t)
+            nc.scalar.activation(v_picked[:], v_raw[t][:].indirect(lists[0][:]), COPY)
+            pairs = v_picked[:].bitcast(F32)
+            turned = ps.tile([P, 2, P], F32, name="bank%d" % (4 + t))
+            for u in range(2):
+                nc.tensor.transpose(turned[:, u, :], pairs[:, u : I // 2 : 2], ident[:])
+            vt_bf = tile([P, P, PACK], BF16, "vt_bf%d" % t)
+            nc.vector.tensor_copy(out=vt_bf[:].bitcast(F32), in_=turned[:].rearrange("p u e -> p e u"))
+            quantize(nc, vt_codes[:, P * t : P * (t + 1)], vt_scales[:, P * t : P * (t + 1)], vt_bf[:])
+
+        y_rows = out_0.rearrange("(p t) q -> p t q", t=PACK)
+        y_scales = tile([P, Q], U8, "y_scales")
+        code_rows = out_1[0].rearrange("p c r -> p (c r)").bitcast(I32)
+
+        def result(h):
+            cols = slice(P * h, P * (h + 1))
+            o = ps.tile([P, PACK, P], F32, name="bank%d" % (2 + h))
+            for t in range(PACK):
+                nc.tensor.matmul_mx(
+                    out=o[:, t, :],
+                    lhsT=vt_codes[:, P * t : P * (t + 1)].bitcast(FP8X4),
+                    lhsT_scale=vt_scales[:, P * t : P * (t + 1)],
+                    rhs=w_codes[:, cols].bitcast(FP8X4),
+                    rhs_scale=w_scales[:, cols],
+                    start=True,
+                    stop=True,
+                )
+            y = tile([P, PACK, P], F32, "y%d" % h)
+            y_bf = tile([P, P, PACK], BF16, "y_bf%d" % h)
+            y_codes = tile([P, P], U32, "y_codes%d" % h)
+            nc.vector.tensor_tensor(y[:], o[:], me_picked[:, :, cols], ALU.mult)
+            nc.sync.dma_start(out=y_rows[:, :, cols], in_=y[:])
+            interleave(nc, y_bf[:], y[:])
+            quantize(nc, y_codes[:], y_scales[:, cols], y_bf[:])
+            nc.scalar.dma_start(out=code_rows[:, cols], in_=y_codes[:].bitcast(I32))
+
         interleave(nc, ms_bf[0][:], ms_raw[0][:])
         quantize(nc, wm_codes[:], wm_scales[:], wm_bf[:])
         quantize(nc, ms_codes[0][:], ms_scales[0][:], ms_bf[0][:])
@@ -187,44 +239,17 @@ def tile_attend_spreadof3_remembered_lean_pl_kernel(
         interleave(nc, ms_bf[1][:], ms_raw[1][:])
         quantize(nc, ms_codes[1][:], ms_scales[1][:], ms_bf[1][:])
         memories(1)
+        values(0)
+        values(1)
         weights(1)
-
-        y = tile([P, PACK, Q], F32, "y")
-        y_rows = out_0.rearrange("(p t) q -> p t q", t=PACK)
-        for t in range(PACK):
-            v_picked = tile([P, I], BF16, "v_picked%d" % t)
-            nc.scalar.activation(me_picked[t][:], me_sb[t][:].indirect(list_mem[:]), COPY)
-            nc.scalar.activation(v_picked[:], v_raw[t][:].indirect(lists[0][:]), COPY)
-            pairs = v_picked[:].bitcast(F32)
-            turned = ps_tr.tile([P, 2, P], F32, name="tr")
-            for u in range(2):
-                nc.tensor.transpose(turned[:, u, :], pairs[:, u : I // 2 : 2], ident[:])
-            vt_bf = tile([P, P, PACK], BF16, "vt_bf%d" % t)
-            vt_codes = tile([P, P], U32, "vt_codes%d" % t)
-            vt_scales = tile([P, P], U8, "vt_scales%d" % t)
-            nc.vector.tensor_copy(out=vt_bf[:].bitcast(F32), in_=turned[:].rearrange("p u e -> p e u"))
-            quantize(nc, vt_codes[:], vt_scales[:], vt_bf[:])
-            o = ps_o.tile([P, Q], F32, name="o")
-            nc.tensor.matmul_mx(
-                out=o[:],
-                lhsT=vt_codes[:].bitcast(FP8X4),
-                lhsT_scale=vt_scales[:],
-                rhs=w_codes[:].bitcast(FP8X4),
-                rhs_scale=w_scales[:],
-                start=True,
-                stop=True,
-            )
-            nc.vector.tensor_tensor(y[:, t, :], o[:], me_picked[t][:], ALU.mult)
-            nc.sync.dma_start(out=y_rows[:, t, :], in_=y[:, t, :])
-
-        y_bf = tile([P, Q, PACK], BF16, "y_bf")
-        y_codes = tile([P, Q], U32, "y_codes")
-        y_scales = tile([P, Q], U8, "y_scales")
-        interleave(nc, y_bf[:], y[:])
-        quantize(nc, y_codes[:], y_scales[:], y_bf[:])
-        nc.scalar.dma_start(
-            out=out_1[0].rearrange("p c r -> p (c r)").bitcast(I32), in_=y_codes[:].bitcast(I32)
-        )
+        values(2)
+        values(3)
+        nc.scalar.activation(me_picked[:, 0, :], me_sb[0][:].indirect(list_mem[:]), COPY)
+        nc.scalar.activation(me_picked[:, 1, :], me_sb[1][:].indirect(list_mem[:]), COPY)
+        nc.scalar.activation(me_picked[:, 2, :], me_sb[2][:].indirect(list_mem[:]), COPY)
+        nc.scalar.activation(me_picked[:, 3, :], me_sb[3][:].indirect(list_mem[:]), COPY)
+        result(0)
+        result(1)
         for g in range(4):
             queue = nc.sync if g % 2 == 0 else nc.scalar
             queue.dma_start(

@@ -42,13 +42,13 @@ def tile_attend_spreadof3_remembered_lean_pl_kernel(
         sb = ctx.enter_context(tc.tile_pool(name="sb", bufs=1))
         ps = ctx.enter_context(tc.psum_pool(name="ps", bufs=1))
 
-        def tile(shape, dtype, name):
-            return sb.tile(shape, dtype, name=name, align_bytes=64)
+        def tile(shape, dtype, name, tag=None):
+            return sb.tile(shape, dtype, name=name, tag=tag or name, align_bytes=64)
 
         lists = [tile([P, I // 16], U16, "list%d" % j) for j in range(3)]
         list_mem = tile([P, Q // 16], U16, "list_mem")
-        q_raw = tile([P, PACK, Q], F32, "q_raw")
-        k_words = tile([P, 2 * T], U8, "k_words")
+        q_raw = [tile([P, PACK, P], F32, "q_raw%d" % h) for h in range(QT)]
+        k_words = [tile([P, T], U8, "k_words%d" % j) for j in range(2)]
         k_scales = tile([P, T], U8, "k_scales")
         wm_raw = tile([P, PACK, E], F32, "wm_raw")
         ms_raw = [tile([P, PACK, BANK], F32, "ms_raw%d" % n) for n in range(M // BANK)]
@@ -58,25 +58,28 @@ def tile_attend_spreadof3_remembered_lean_pl_kernel(
         ident = tile([P, P], F32, "ident")
 
         nc.vector.memset(k_scales[:].bitcast(I32), 0)
-        nc.sync.dma_start(out=q_raw[:], in_=query.rearrange("(p t) q -> p t q", t=PACK))
-        nc.sync.dma_start(out=k_words[:].bitcast(I32), in_=keys_words[0].bitcast(I32))
+        q_rows = query.rearrange("(p t) q -> p t q", t=PACK)
+        nc.sync.dma_start(out=q_raw[0][:], in_=q_rows[:, :, 0:P])
+        nc.sync.dma_start(out=k_words[0][:].bitcast(I32), in_=keys_words[0, :, 0:T].bitcast(I32))
         for g in range(4):
             nc.sync.dma_start(
                 out=k_scales[32 * g : 32 * g + 4, :].bitcast(I32), in_=keys_scales[0, 4 * g : 4 * g + 4, :].bitcast(I32)
             )
+        nc.sync.dma_start(out=k_words[1][:].bitcast(I32), in_=keys_words[0, :, T : 2 * T].bitcast(I32))
+        nc.sync.dma_start(out=q_raw[1][:], in_=q_rows[:, :, P : 2 * P])
         with nc.allow_non_contiguous_dma(reason="one factor a partition"):
             nc.gpsimd.dma_start(out=lam_raw[:], in_=lam.rearrange("(h p) o -> p (h o)", p=P))
         nc.gpsimd.dma_start(out=os_raw[:], in_=slot_factor.rearrange("o (p t) -> p (o t)", t=PACK))
         make_identity(nc, ident[:])
         ms_rows = mstore.rearrange("(p t) m -> p t m", t=PACK)
         v_rows = vals.rearrange("(p t) x -> p t x", t=PACK)
-        nc.sync.dma_start(out=wm_raw[:], in_=wm.rearrange("(p t) e -> p t e", t=PACK))
         for dst, src in zip(lists, (offs, offs2, offs3)):
             nc.sync.dma_start(dst[:], src)
+        nc.sync.dma_start(out=wm_raw[:], in_=wm.rearrange("(p t) e -> p t e", t=PACK))
         nc.sync.dma_start(out=ms_raw[0][:], in_=ms_rows[:, :, 0 * BANK : (0 + 1) * BANK])
-        nc.sync.dma_start(out=v_raw[0][:], in_=v_rows[:, 0, :])
         nc.sync.dma_start(out=ms_raw[1][:], in_=ms_rows[:, :, 1 * BANK : (1 + 1) * BANK])
         nc.sync.dma_start(list_mem[:], offs4)
+        nc.sync.dma_start(out=v_raw[0][:], in_=v_rows[:, 0, :])
         nc.sync.dma_start(out=v_raw[1][:], in_=v_rows[:, 1, :])
         nc.sync.dma_start(out=v_raw[2][:], in_=v_rows[:, 2, :])
         nc.sync.dma_start(out=v_raw[3][:], in_=v_rows[:, 3, :])
@@ -92,7 +95,7 @@ def tile_attend_spreadof3_remembered_lean_pl_kernel(
         q_codes = [tile([P, P], U32, "q_codes%d" % h) for h in range(QT)]
         q_scales = [tile([P, P], U8, "q_scales%d" % h) for h in range(QT)]
         for h in range(QT):
-            interleave(nc, q_bf[h][:], q_raw[:, :, h * P : (h + 1) * P])
+            interleave(nc, q_bf[h][:], q_raw[h][:])
         for h in range(QT):
             quantize(nc, q_codes[h][:], q_scales[h][:], q_bf[h][:])
 
@@ -105,13 +108,13 @@ def tile_attend_spreadof3_remembered_lean_pl_kernel(
                     out=bank[:],
                     lhsT=q_codes[h][:].bitcast(FP8X4),
                     lhsT_scale=q_scales[h][:],
-                    rhs=k_words[:, 2 * BANK * n : 2 * BANK * (n + 1)].bitcast(FP4X4),
+                    rhs=k_words[n // 2][:, 2 * BANK * (n % 2) : 2 * BANK * (n % 2 + 1)].bitcast(FP4X4),
                     rhs_scale=k_scales[:, BANK * n : BANK * (n + 1)],
                     start=True,
                     stop=True,
                 )
                 dst = a_sb[h][:, BANK * n : BANK * (n + 1)]
-                if h == 0 and n % 2 == 0:
+                if h == 0:
                     nc.scalar.activation(dst, bank[:], COPY)
                 else:
                     nc.vector.tensor_copy(dst, bank[:])
@@ -129,7 +132,6 @@ def tile_attend_spreadof3_remembered_lean_pl_kernel(
         ms_codes = [tile([P, BANK], U32, "ms_codes%d" % n) for n in range(M // BANK)]
         ms_scales = [tile([P, BANK], U8, "ms_scales%d" % n) for n in range(M // BANK)]
         me_sb = [tile([P, M], F32, "me_sb%d" % t) for t in range(PACK)]
-        me_picked = tile([P, PACK, Q], F32, "me_picked")
 
         def memories(n):
             for t in range(PACK):
@@ -155,22 +157,22 @@ def tile_attend_spreadof3_remembered_lean_pl_kernel(
 
         def weights(h):
             g1, g2, g3 = picked[h]
-            hi2 = tile([P, I], F32, "hi2_%d" % h)
-            lo2 = tile([P, I], F32, "lo2_%d" % h)
+            ends2 = tile([P, 2, I], F32, "ends2_%d" % h, tag="ms_bf1")
+            hi2, lo2 = ends2[:, 0, :], ends2[:, 1, :]
             hi3 = tile([P, I], F32, "hi3_%d" % h)
             lo3 = tile([P, I], F32, "lo3_%d" % h)
             up = tile([P, PACK, P], F32, "up_%d" % h)
             down = tile([P, PACK, P], F32, "down_%d" % h)
-            nc.vector.tensor_tensor(hi2[:], g1[:], g2[:], ALU.max)
-            nc.vector.tensor_tensor(lo2[:], g1[:], g2[:], ALU.min)
-            nc.vector.tensor_tensor(hi3[:], hi2[:], g3[:], ALU.max)
-            nc.vector.tensor_tensor(lo3[:], lo2[:], g3[:], ALU.min)
+            nc.vector.tensor_tensor(hi2, g1[:], g2[:], ALU.max)
+            nc.vector.tensor_tensor(lo2, g1[:], g2[:], ALU.min)
+            nc.vector.tensor_tensor(hi3[:], hi2, g3[:], ALU.max)
+            nc.vector.tensor_tensor(lo3[:], lo2, g3[:], ALU.min)
             for term, end3, factor, end2 in ((up, hi3, lam_neg, hi2), (down, lo3, lam_pos, lo2)):
                 nc.vector.scalar_tensor_tensor(
                     term[:].rearrange("p r s -> p s r"),
                     end3[:].rearrange("p (s r) -> p s r", r=PACK),
                     factor[:, h : h + 1],
-                    end2[:].rearrange("p (s r) -> p s r", r=PACK),
+                    end2.rearrange("p (s r) -> p s r", r=PACK),
                     ALU.mult,
                     ALU.add,
                 )
@@ -225,9 +227,14 @@ def tile_attend_spreadof3_remembered_lean_pl_kernel(
             y = tile([P, PACK, P], F32, "y%d" % h)
             y_bf = tile([P, P, PACK], BF16, "y_bf%d" % h)
             y_codes = tile([P, P], U32, "y_codes%d" % h)
-            nc.vector.tensor_tensor(y[:], o[:], me_picked[:, :, cols], ALU.mult)
+            nc.vector.tensor_tensor(y[:], o[:], me_picked[:, h], ALU.mult)
             nc.sync.dma_start(out=y_rows[:, :, cols], in_=y[:])
-            interleave(nc, y_bf[:], y[:])
+            if h == 0:
+                nc.scalar.copy(
+                    out=y_bf[:].rearrange("p (c i) t -> p c t i", i=4), in_=y[:].rearrange("p t (c i) -> p c t i", i=4)
+                )
+            else:
+                interleave(nc, y_bf[:], y[:])
             quantize(nc, y_codes[:], y_scales[:, cols], y_bf[:])
             nc.scalar.dma_start(out=code_rows[:, cols], in_=y_codes[:].bitcast(I32))
 
@@ -235,19 +242,20 @@ def tile_attend_spreadof3_remembered_lean_pl_kernel(
         quantize(nc, wm_codes[:], wm_scales[:], wm_bf[:])
         quantize(nc, ms_codes[0][:], ms_scales[0][:], ms_bf[0][:])
         memories(0)
-        weights(0)
         interleave(nc, ms_bf[1][:], ms_raw[1][:])
         quantize(nc, ms_codes[1][:], ms_scales[1][:], ms_bf[1][:])
         memories(1)
+        weights(0)
+        weights(1)
         values(0)
         values(1)
-        weights(1)
         values(2)
         values(3)
-        nc.scalar.activation(me_picked[:, 0, :], me_sb[0][:].indirect(list_mem[:]), COPY)
-        nc.scalar.activation(me_picked[:, 1, :], me_sb[1][:].indirect(list_mem[:]), COPY)
-        nc.scalar.activation(me_picked[:, 2, :], me_sb[2][:].indirect(list_mem[:]), COPY)
-        nc.scalar.activation(me_picked[:, 3, :], me_sb[3][:].indirect(list_mem[:]), COPY)
+        me_picked = tile([P, QT, PACK, P], F32, "me_picked", tag="v_raw3")
+        for h in range(QT):
+            for t in range(PACK):
+                rows = list_mem[:, h * (P // 16) : (h + 1) * (P // 16)]
+                nc.scalar.activation(me_picked[:, h, t, :], me_sb[t][:].indirect(rows), COPY)
         result(0)
         result(1)
         for g in range(4):

from contextlib import ExitStack

import concourse.mybir as mybir
from concourse.masks import make_identity

D, T, I, Q, E, M, C = 512, 2048, 512, 256, 512, 1024, 512
FLOPS = 2 * (D * Q * T + I * E * Q + C * E * M)

F32 = mybir.dt.float32
BF16 = mybir.dt.bfloat16
I32 = mybir.dt.int32
U32 = mybir.dt.uint32
U16 = mybir.dt.uint16
U8 = mybir.dt.uint8
FP8X4 = mybir.dt.float8_e4m3fn_x4
FP4X4 = mybir.dt.float4_e2m1fn_x4
ALU = mybir.AluOpType
COPY = mybir.ActivationFunctionType.Copy

P = 128
PACK = 4
BANK = 512
QT = Q // P


def interleave(nc, grouped, raw):
    nc.vector.tensor_copy(
        out=grouped.rearrange("p (c i) t -> p c t i", i=4),
        in_=raw.rearrange("p t (c i) -> p c t i", i=4),
    )


def quantize(nc, codes, scales, grouped):
    nc.vector.quantize_mx(out=codes.bitcast(FP8X4), scales=scales, in_=grouped.rearrange("p c t -> p (c t)"))


def tile_attend_spreadof3_remembered_lean_pl_kernel(
    tc, query, keys_words, keys_scales, lam, slot_factor, vals, wm, mstore, offs, offs2, offs3, offs4, out_0, out_1, out_2
):
    nc = tc.nc
    with ExitStack() as ctx:
        sb = ctx.enter_context(tc.tile_pool(name="sb", bufs=1))
        ps = ctx.enter_context(tc.psum_pool(name="ps", bufs=1))

        def tile(shape, dtype, name, tag=None):
            return sb.tile(shape, dtype, name=name, tag=tag or name, align_bytes=64)

        lists = [tile([P, I // 16], U16, "list%d" % j) for j in range(3)]
        list_mem = tile([P, Q // 16], U16, "list_mem")
        q_raw = [tile([P, PACK, P], F32, "q_raw%d" % h) for h in range(QT)]
        k_words = [tile([P, T], U8, "k_words%d" % j) for j in range(2)]
        k_scales = tile([P, T], U8, "k_scales")
        wm_raw = tile([P, PACK, E], F32, "wm_raw")
        ms_raw = [tile([P, PACK, BANK], F32, "ms_raw%d" % n) for n in range(M // BANK)]
        v_raw = [tile([P, T], F32, "v_raw%d" % t) for t in range(PACK)]
        lam_raw = tile([P, QT], F32, "lam_raw")
        os_raw = tile([P, PACK], F32, "os_raw")
        ident = tile([P, P], F32, "ident")

        nc.vector.memset(k_scales[:].bitcast(I32), 0)
        q_rows = query.rearrange("(p t) q -> p t q", t=PACK)
        nc.sync.dma_start(out=q_raw[0][:], in_=q_rows[:, :, 0:P])
        nc.sync.dma_start(out=k_words[0][:].bitcast(I32), in_=keys_words[0, :, 0:T].bitcast(I32))
        for g in range(4):
            nc.sync.dma_start(
                out=k_scales[32 * g : 32 * g + 4, :].bitcast(I32), in_=keys_scales[0, 4 * g : 4 * g + 4, :].bitcast(I32)
            )
        nc.sync.dma_start(out=k_words[1][:].bitcast(I32), in_=keys_words[0, :, T : 2 * T].bitcast(I32))
        nc.sync.dma_start(out=q_raw[1][:], in_=q_rows[:, :, P : 2 * P])
        with nc.allow_non_contiguous_dma(reason="one factor a partition"):
            nc.gpsimd.dma_start(out=lam_raw[:], in_=lam.rearrange("(h p) o -> p (h o)", p=P))
        nc.gpsimd.dma_start(out=os_raw[:], in_=slot_factor.rearrange("o (p t) -> p (o t)", t=PACK))
        make_identity(nc, ident[:])
        ms_rows = mstore.rearrange("(p t) m -> p t m", t=PACK)
        v_rows = vals.rearrange("(p t) x -> p t x", t=PACK)
        for dst, src in zip(lists, (offs, offs2, offs3)):
            nc.sync.dma_start(dst[:], src)
        nc.sync.dma_start(out=wm_raw[:], in_=wm.rearrange("(p t) e -> p t e", t=PACK))
        nc.sync.dma_start(out=ms_raw[0][:], in_=ms_rows[:, :, 0 * BANK : (0 + 1) * BANK])
        nc.sync.dma_start(out=ms_raw[1][:], in_=ms_rows[:, :, 1 * BANK : (1 + 1) * BANK])
        nc.sync.dma_start(list_mem[:], offs4)
        nc.sync.dma_start(out=v_raw[0][:], in_=v_rows[:, 0, :])
        nc.sync.dma_start(out=v_raw[1][:], in_=v_rows[:, 1, :])
        nc.sync.dma_start(out=v_raw[2][:], in_=v_rows[:, 2, :])
        nc.sync.dma_start(out=v_raw[3][:], in_=v_rows[:, 3, :])

        lam_neg = tile([P, QT], F32, "lam_neg")
        lam_pos = tile([P, QT], F32, "lam_pos")
        os_third = tile([P, PACK], F32, "os_third")
        nc.gpsimd.tensor_scalar(lam_neg[:], lam_raw[:], -3.0, 0.0, ALU.mult, ALU.add)
        nc.gpsimd.tensor_scalar(lam_pos[:], lam_raw[:], 3.0, 0.0, ALU.mult, ALU.add)
        nc.gpsimd.tensor_scalar(os_third[:], os_raw[:], 1.0 / 3.0, 0.0, ALU.mult, ALU.add)

        q_bf = [tile([P, P, PACK], BF16, "q_bf%d" % h) for h in range(QT)]
        q_codes = [tile([P, P], U32, "q_codes%d" % h) for h in range(QT)]
        q_scales = [tile([P, P], U8, "q_scales%d" % h) for h in range(QT)]
        for h in range(QT):
            interleave(nc, q_bf[h][:], q_raw[h][:])
        for h in range(QT):
            quantize(nc, q_codes[h][:], q_scales[h][:], q_bf[h][:])

        a_sb = [tile([P, T], F32, "a_sb%d" % h) for h in range(QT)]
        picked = [[tile([P, I], F32, "picked%d_%d" % (h, j)) for j in range(3)] for h in range(QT)]
        for h in range(QT):
            for n in range(T // BANK):
                bank = ps.tile([P, BANK], F32, name="bank%d" % (4 * h + n))
                nc.tensor.matmul_mx(
                    out=bank[:],
                    lhsT=q_codes[h][:].bitcast(FP8X4),
                    lhsT_scale=q_scales[h][:],
                    rhs=k_words[n // 2][:, 2 * BANK * (n % 2) : 2 * BANK * (n % 2 + 1)].bitcast(FP4X4),
                    rhs_scale=k_scales[:, BANK * n : BANK * (n + 1)],
                    start=True,
                    stop=True,
                )
                dst = a_sb[h][:, BANK * n : BANK * (n + 1)]
                if h == 0:
                    nc.scalar.activation(dst, bank[:], COPY)
                else:
                    nc.vector.tensor_copy(dst, bank[:])
            for j in range(3):
                nc.scalar.activation(picked[h][j][:], a_sb[h][:].indirect(lists[j][:]), COPY)

        wm_bf = tile([P, E, PACK], BF16, "wm_bf")
        wm_codes = tile([P, E], U32, "wm_codes")
        wm_scales = tile([P, E], U8, "wm_scales")
        nc.vector.tensor_copy(
            out=wm_bf[:].rearrange("p (t m) j -> p m j t", t=PACK),
            in_=wm_raw[:].rearrange("p j (m t) -> p m j t", t=PACK),
        )
        ms_bf = [tile([P, BANK, PACK], BF16, "ms_bf%d" % n) for n in range(M // BANK)]
        ms_codes = [tile([P, BANK], U32, "ms_codes%d" % n) for n in range(M // BANK)]
        ms_scales = [tile([P, BANK], U8, "ms_scales%d" % n) for n in range(M // BANK)]
        me_sb = [tile([P, M], F32, "me_sb%d" % t) for t in range(PACK)]

        def memories(n):
            for t in range(PACK):
                bank = ps.tile([P, BANK], F32, name="bank%d" % (4 * n + t))
                nc.tensor.matmul_mx(
                    out=bank[:],
                    lhsT=wm_codes[:, P * t : P * (t + 1)].bitcast(FP8X4),
                    lhsT_scale=wm_scales[:, P * t : P * (t + 1)],
                    rhs=ms_codes[n][:].bitcast(FP8X4),
                    rhs_scale=ms_scales[n][:],
                    start=True,
                    stop=True,
                )
                dst = me_sb[t][:, BANK * n : BANK * (n + 1)]
                if True:
                    nc.scalar.activation(dst, bank[:], COPY)
                else:
                    nc.vector.tensor_copy(dst, bank[:])

        w_bf = [tile([P, P, PACK], BF16, "w_bf%d" % h) for h in range(QT)]
        w_codes = tile([P, Q], U32, "w_codes")
        w_scales = tile([P, Q], U8, "w_scales")

        def weights(h):
            g1, g2, g3 = picked[h]
            ends2 = tile([P, 2, I], F32, "ends2_%d" % h, tag="ms_bf1")
            hi2, lo2 = ends2[:, 0, :], ends2[:, 1, :]
            hi3 = tile([P, I], F32, "hi3_%d" % h)
            lo3 = tile([P, I], F32, "lo3_%d" % h)
            up = tile([P, PACK, P], F32, "up_%d" % h)
            down = tile([P, PACK, P], F32, "down_%d" % h)
            nc.vector.tensor_tensor(hi2, g1[:], g2[:], ALU.max)
            nc.vector.tensor_tensor(lo2, g1[:], g2[:], ALU.min)
            nc.vector.tensor_tensor(hi3[:], hi2, g3[:], ALU.max)
            nc.vector.tensor_tensor(lo3[:], lo2, g3[:], ALU.min)
            for term, end3, factor, end2 in ((up, hi3, lam_neg, hi2), (down, lo3, lam_pos, lo2)):
                nc.vector.scalar_tensor_tensor(
                    term[:].rearrange("p r s -> p s r"),
                    end3[:].rearrange("p (s r) -> p s r", r=PACK),
                    factor[:, h : h + 1],
                    end2.rearrange("p (s r) -> p s r", r=PACK),
                    ALU.mult,
                    ALU.add,
                )
            bank = ps.tile([P, PACK, P], F32, name="bank%d" % (h))
            terms = [(r, up[:, r, :]) for r in range(PACK)] + [(r, g3[:, r:I:PACK]) for r in range(PACK)]
            terms = terms + [(r, down[:, r, :]) for r in range(PACK)]
            for j, (r, term) in enumerate(terms):
                nc.tensor.matmul(
                    bank[:, r, :], term, ident[:], start=(j == 0), stop=(j == len(terms) - 1), is_transpose=True
                )
            nc.vector.scalar_tensor_tensor(
                w_bf[h][:],
                bank[:].rearrange("p r q -> p q r"),
                0.0,
                os_third[:].unsqueeze(1).to_broadcast([P, P, PACK]),
                ALU.max,
                ALU.mult,
            )
            quantize(nc, w_codes[:, P * h : P * (h + 1)], w_scales[:, P * h : P * (h + 1)], w_bf[h][:])

        vt_codes = tile([P, E], U32, "vt_codes")
        vt_scales = tile([P, E], U8, "vt_scales")

        def values(t):
            v_picked = tile([P, I], BF16, "v_picked%d" % t)
            nc.scalar.activation(v_picked[:], v_raw[t][:].indirect(lists[0][:]), COPY)
            pairs = v_picked[:].bitcast(F32)
            turned = ps.tile([P, 2, P], F32, name="bank%d" % (4 + t))
            for u in range(2):
                nc.tensor.transpose(turned[:, u, :], pairs[:, u : I // 2 : 2], ident[:])
            vt_bf = tile([P, P, PACK], BF16, "vt_bf%d" % t)
            nc.vector.tensor_copy(out=vt_bf[:].bitcast(F32), in_=turned[:].rearrange("p u e -> p e u"))
            quantize(nc, vt_codes[:, P * t : P * (t + 1)], vt_scales[:, P * t : P * (t + 1)], vt_bf[:])

        y_rows = out_0.rearrange("(p t) q -> p t q", t=PACK)
        y_scales = tile([P, Q], U8, "y_scales")
        code_rows = out_1[0].rearrange("p c r -> p (c r)").bitcast(I32)

        def result(h):
            cols = slice(P * h, P * (h + 1))
            o = ps.tile([P, PACK, P], F32, name="bank%d" % (2 + h))
            for t in range(PACK):
                nc.tensor.matmul_mx(
                    out=o[:, t, :],
                    lhsT=vt_codes[:, P * t : P * (t + 1)].bitcast(FP8X4),
                    lhsT_scale=vt_scales[:, P * t : P * (t + 1)],
                    rhs=w_codes[:, cols].bitcast(FP8X4),
                    rhs_scale=w_scales[:, cols],
                    start=True,
                    stop=True,
                )
            y = tile([P, PACK, P], F32, "y%d" % h)
            y_bf = tile([P, P, PACK], BF16, "y_bf%d" % h)
            y_codes = tile([P, P], U32, "y_codes%d" % h)
            nc.vector.tensor_tensor(y[:], o[:], me_picked[:, h], ALU.mult)
            nc.sync.dma_start(out=y_rows[:, :, cols], in_=y[:])
            if h == 0:
                nc.scalar.copy(
                    out=y_bf[:].rearrange("p (c i) t -> p c t i", i=4), in_=y[:].rearrange("p t (c i) -> p c t i", i=4)
                )
            else:
                interleave(nc, y_bf[:], y[:])
            quantize(nc, y_codes[:], y_scales[:, cols], y_bf[:])
            nc.scalar.dma_start(out=code_rows[:, cols], in_=y_codes[:].bitcast(I32))

        interleave(nc, ms_bf[0][:], ms_raw[0][:])
        quantize(nc, wm_codes[:], wm_scales[:], wm_bf[:])
        quantize(nc, ms_codes[0][:], ms_scales[0][:], ms_bf[0][:])
        memories(0)
        interleave(nc, ms_bf[1][:], ms_raw[1][:])
        quantize(nc, ms_codes[1][:], ms_scales[1][:], ms_bf[1][:])
        memories(1)
        weights(0)
        weights(1)
        values(0)
        values(1)
        values(2)
        values(3)
        me_picked = tile([P, QT, PACK, P], F32, "me_picked", tag="v_raw3")
        for h in range(QT):
            for t in range(PACK):
                rows = list_mem[:, h * (P // 16) : (h + 1) * (P // 16)]
                nc.scalar.activation(me_picked[:, h, t, :], me_sb[t][:].indirect(rows), COPY)
        result(0)
        result(1)
        for g in range(4):
            queue = nc.sync if g % 2 == 0 else nc.scalar
            queue.dma_start(
                out=out_2[0, 4 * g : 4 * g + 4, :].bitcast(I32), in_=y_scales[32 * g : 32 * g + 4, :].bitcast(I32)
            )
